import numpy as np
import ml_dtypes


def mxq(x, axis, fmt="e4m3"):
    dtype, down = {"e4m3": (ml_dtypes.float8_e4m3fn, 7), "e5m2": (ml_dtypes.float8_e5m2, 14)}[fmt]
    v = np.moveaxis(np.asarray(x, np.float32).astype(ml_dtypes.bfloat16).astype(np.float64), axis, -1)
    blocks = v.reshape(v.shape[:-1] + (-1, 32))
    amax = np.abs(blocks).max(-1, keepdims=True)
    byte = np.maximum(np.where(amax > 0, np.frexp(amax)[1] - 1 + 127, 0) - down, 1)
    scale = np.exp2(byte - 127.0)
    codes = (blocks / scale).astype(np.float32).astype(dtype).astype(np.float64)
    return np.moveaxis((codes * scale).reshape(v.shape), -1, axis)


WIDE = False


def mx_kscale(k):
    if not WIDE:
        return np.ones(k)
    levels = np.array([10, -10, 5, -5, 0])
    if k % 512:
        return np.exp2(np.random.permutation(np.resize(levels, k // 32))).repeat(32)
    a = np.empty((k // 512, 16))
    for p in range(k // 512):
        a[p, :8] = np.random.permutation(np.resize(levels, 8))
        for g in range(8):
            far = levels[np.abs(levels - a[p, g]) >= 10]
            a[p, g + 8] = far[np.random.randint(len(far))]
    return np.exp2(a.ravel()).repeat(32)


def f64(x):
    return np.asarray(x).astype(np.float64)


def striped(idx):
    return np.tile(np.asarray(idx).reshape(-1, 16).T, (8, 1)).astype(np.uint16)


def unstriped(offs):
    return offs[:16].T.reshape(-1).astype(np.int64)


E2M1 = np.array([0.0, 0.5, 1.0, 1.5, 2.0, 3.0, 4.0, 6.0, -0.0, -0.5, -1.0, -1.5, -2.0, -3.0, -4.0, -6.0])


def pack_weight(w, fmt):
    k, n = w.shape
    w = f64(np.asarray(w, np.float32).astype(ml_dtypes.bfloat16)).reshape(k // 32, 32, n)
    amax = np.abs(w).max(1)
    if fmt == "e4m3":
        byte = np.frexp(amax)[1] - 1 + 127 - 7
    else:
        mant, ex = np.frexp(amax / 6.0)
        byte = np.where(mant > 0.5, ex, ex - 1) + 127
    byte = np.clip(np.where(amax > 0, byte, 1), 1, 254)
    scaled = (w * np.exp2(127.0 - byte)[:, None, :]).reshape(k, n).astype(np.float32)
    by_word = np.ascontiguousarray(scaled.reshape(k // 512, 128, 4, n).transpose(0, 1, 3, 2))
    if fmt == "e4m3":
        words = by_word.astype(ml_dtypes.float8_e4m3fn).view(np.uint8)
    else:
        c = by_word.astype(ml_dtypes.float4_e2m1fn).view(np.uint8) & 0xF
        words = (c[..., 0::2] | (c[..., 1::2] << 4)).reshape(k // 512, 128, 2 * n)
    return np.ascontiguousarray(words), np.ascontiguousarray(byte.astype(np.uint8).reshape(k // 512, 16, n))


def unpack_weight(words, scales, fmt):
    g, _, n = scales.shape
    words = np.ascontiguousarray(words).reshape(g, 128, n, -1)
    if fmt == "e4m3":
        vals = words.view(ml_dtypes.float8_e4m3fn).astype(np.float64)
    else:
        nib = np.empty((g, 128, n, 4), np.uint8)
        nib[..., 0::2] = words & 0xF
        nib[..., 1::2] = words >> 4
        vals = E2M1[nib]
    vals = vals * np.repeat(np.exp2(scales.astype(np.float64) - 127.0), 8, axis=1)[..., None]
    return vals.transpose(0, 1, 3, 2).reshape(g * 512, n)


def softplus(v):
    return np.log(1.0 + np.exp(v))


D, T, I, Q, M = 512, 2048, 512, 128, 2048


def setup_inputs():
    n = np.random.standard_normal
    idx = np.random.permutation(T)[:I]
    idx2 = np.random.permutation(M)[:I]
    idx4 = np.random.permutation(I)[:I]
    fd = mx_kscale(D)
    keysp = pack_weight(n((D, T)) / fd[:, None], "e4m3")
    return {
        "query": (n((D, Q)) * 1.0 / np.sqrt(D) * fd[:, None]).astype(np.float32),
        "keys_words": keysp[0],
        "keys_scales": keysp[1],
        "ceil_t": np.tile(np.random.uniform(1.0, 4.0, T), (128, 1)).astype(np.float32),
        "halfp": np.tile(np.random.uniform(0.4, 1.5, T), (128, 1)).astype(np.float32),
        "rival": (np.random.uniform(0.5, 2.0, (Q, 1))).astype(np.float32),
        "old": (np.random.uniform(0.0, 2.0, (Q, M))).astype(np.float32),
        "fade": (np.random.uniform(0.3, 0.9, (Q, 1))).astype(np.float32),
        "offs": striped(idx),
        "offs2": striped(idx2),
        "offs4": striped(idx4),
    }


def reference(query, keys_words, keys_scales, ceil_t, halfp, rival, old, fade, offs, offs2, offs4):
    idx = unstriped(offs)
    idx2 = unstriped(offs2)
    idx4 = unstriped(offs4)
    keysu = unpack_weight(keys_words, keys_scales, "e4m3")
    queryq = mxq(f64(query), 0, "e4m3")
    keysidxg = keysu[:, idx]
    a = queryq.T @ keysidxg
    fa = softplus(a * 2.0)
    s = fa * f64(ceil_t)[:1][:, idx] / (fa + f64(halfp)[:1][:, idx])
    p = np.exp(s)
    r = p / (p + p[:, idx4] * f64(rival))
    w = r / np.sum(r, axis=1, keepdims=True)
    ws = w * 512.0
    wf = np.zeros((Q, M))
    wf[:, idx2] = ws
    y = f64(old) * f64(fade) + wf
    return y

@@ -1,0 +1,166 @@
+from contextlib import ExitStack
+
+import concourse.mybir as mybir
+
+D, T, I, Q, M = 512, 2048, 512, 128, 2048
+FLOPS = 2 * D * Q * I
+
+F32 = mybir.dt.float32
+BF16 = mybir.dt.bfloat16
+I32 = mybir.dt.int32
+U32 = mybir.dt.uint32
+U16 = mybir.dt.uint16
+U8 = mybir.dt.uint8
+FP8X4 = mybir.dt.float8_e4m3fn_x4
+ALU = mybir.AluOpType
+ACT = mybir.ActivationFunctionType
+
+P = 128
+PACK = 4
+HALF = I // 2
+HALVES = [slice(0, HALF), slice(HALF, I)]
+LIST_HALVES = [slice(0, HALF // 16), slice(HALF // 16, I // 16)]
+OVERLAP = 16
+STAGGERED = [slice(0, HALF + OVERLAP), slice(HALF + OVERLAP, I)]
+KNEE = 40.0
+OUT_CHUNKS = 4
+CHUNK = M // OUT_CHUNKS
+STORE_EDGES = [0, 256, 768, 1280, 1792, M]
+
+
+def tile_attend_saturating_overlinked_counts_kernel(
+    tc, query, keys_words, keys_scales, ceil_t, halfp, rival, old, fade, offs, offs2, offs4, out
+):
+    nc = tc.nc
+    with ExitStack() as ctx:
+        lists = ctx.enter_context(tc.tile_pool(name="lists", bufs=1))
+        pool = ctx.enter_context(tc.tile_pool(name="work", bufs=1))
+        psum = ctx.enter_context(tc.psum_pool(name="psum", bufs=1))
+
+        idx = lists.tile([P, I // 16], U16, name="idx")
+        idx2 = lists.tile([P, I // 16], U16, name="idx2")
+        idx4 = lists.tile([P, I // 16], U16, name="idx4")
+        words = pool.tile([P, T], U32, name="words", align_bytes=64, tag="words_then_old")
+        scales = pool.tile([P, T], U8, name="scales", align_bytes=64, tag="bytes_then_words0")
+        q_raw = pool.tile([P, PACK, Q], F32, name="q_raw", tag="query_then_ceil")
+        placed = pool.tile([P, M], F32, name="placed")
+        zero = pool.tile([P, 1], F32, name="zero")
+        unit = pool.tile([P, 1], F32, name="unit")
+        one = pool.tile([P, 1], F32, name="one")
+
+        nc.vector.memset(scales[:].bitcast(I32), 0)
+        nc.vector.memset(zero[:], 0.0)
+        nc.vector.memset(unit[:], -1.0)
+        nc.vector.memset(placed[:], 0.0)
+
+        nc.sync.dma_start(idx[:], offs)
+        nc.sync.dma_start(idx4[:], offs4)
+        nc.sync.dma_start(q_raw[:], query.rearrange("(p j) q -> p j q", j=PACK))
+        nc.sync.dma_start(words[:].bitcast(I32), keys_words[0].rearrange("p n t -> p (n t)").bitcast(I32))
+        for quad, queue in enumerate((nc.scalar, nc.scalar, nc.scalar, nc.scalar)):
+            queue.dma_start(
+                scales[:].bitcast(I32)[32 * quad : 32 * quad + 4, :],
+                keys_scales[0, 4 * quad : 4 * quad + 4, :].bitcast(I32),
+            )
+        nc.sync.dma_start(idx2[:], offs2)
+        half_pts = pool.tile([P, T], F32, name="half_pts")
+        nc.sync.dma_start(half_pts[:], halfp)
+
+        nc.scalar.activation(one[:], zero[:], ACT.Exp)
+
+        q_bf = pool.tile([P, Q, PACK], BF16, name="q_bf", align_bytes=64)
+        nc.vector.tensor_scalar(q_bf[:], q_raw[:].rearrange("p j q -> p q j"), 2.0, None, ALU.mult)
+        ceilings = pool.tile([P, T], F32, name="ceilings", tag="query_then_ceil")
+        nc.sync.dma_start(ceilings[:], ceil_t)
+        q_codes = pool.tile([P, Q], U32, name="q_codes", align_bytes=64, tag="codes_then_rival")
+        q_scales = pool.tile([P, Q], U8, name="q_scales", align_bytes=64, tag="bytes_then_fade")
+        k_scales = pool.tile([P, I], U8, name="k_scales", align_bytes=64)
+        nc.vector.quantize_mx(
+            out=q_codes[:].bitcast(FP8X4), scales=q_scales[:], in_=q_bf[:].rearrange("p q j -> p (q j)")
+        )
+
+        nc.vector.tensor_copy(k_scales[:], scales[:].indirect(idx[:]))
+        x = []
+        for h in range(2):
+            k_words = pool.tile([P, HALF], U32, name=f"k_words{h}", align_bytes=64, tag=f"bytes_then_words{h}")
+            nc.vector.tensor_copy(k_words[:], words[:].indirect(idx[:, LIST_HALVES[h]]))
+            bank = psum.tile([P, HALF], F32, name=f"x{h}")
+            nc.tensor.matmul_mx(
+                out=bank[:],
+                lhsT=q_codes[:].bitcast(FP8X4),
+                lhsT_scale=q_scales[:],
+                rhs=k_words[:].bitcast(FP8X4),
+                rhs_scale=k_scales[:, HALVES[h]],
+                start=True,
+                stop=True,
+            )
+            x.append(bank)
+
+        rival_sb = pool.tile([P, 1], F32, name="rival_sb", align_bytes=64, tag="codes_then_rival")
+        fade_sb = pool.tile([P, 1], F32, name="fade_sb", align_bytes=64, tag="bytes_then_fade")
+        nc.sync.dma_start(rival_sb[:], rival)
+        nc.sync.dma_start(fade_sb[:], fade)
+        old_sb = pool.tile([P, M], F32, name="old_sb", align_bytes=64, tag="words_then_old")
+        nc.sync.dma_start(old_sb[:], old)
+
+        def slots(name):
+            return pool.tile([P, I], F32, name=name)
+
+        ex, soft, excess, half_plus, denom = (slots(n) for n in ("ex", "soft", "excess", "half_plus", "denom"))
+        ln_denom, inv_denom, fa, numer, s = (slots(n) for n in ("ln_denom", "inv_denom", "fa", "numer", "s"))
+        p, inv_p, ratio, root = (slots(n) for n in ("p", "inv_p", "ratio", "root"))
+
+        for h in range(2):
+            nc.scalar.activation(ex[:, HALVES[h]], x[h][:], ACT.Exp)
+        for h in range(2):
+            nc.vector.tensor_scalar(excess[:, HALVES[h]], x[h][:], -KNEE, 0.0, ALU.add, ALU.max)
+            nc.vector.tensor_tensor(
+                half_plus[:, HALVES[h]], half_pts[:].indirect(idx[:, LIST_HALVES[h]]), excess[:, HALVES[h]], ALU.add
+            )
+        for cols in STAGGERED:
+            nc.scalar.activation(soft[:, cols], ex[:, cols], ACT.Ln, bias=one[:])
+        for cols in HALVES:
+            nc.vector.scalar_tensor_tensor(denom[:, cols], soft[:, cols], KNEE, half_plus[:, cols], ALU.min, ALU.add)
+            nc.scalar.activation(ln_denom[:, cols], denom[:, cols], ACT.Ln)
+        nc.vector.scalar_tensor_tensor(fa[:], soft[:], KNEE, excess[:], ALU.min, ALU.add)
+        for h in range(2):
+            nc.vector.tensor_tensor(
+                numer[:, HALVES[h]], ceilings[:].indirect(idx[:, LIST_HALVES[h]]), fa[:, HALVES[h]], ALU.mult
+            )
+        for cols in STAGGERED:
+            nc.scalar.activation(inv_denom[:, cols], ln_denom[:, cols], ACT.Exp, scale=-1.0)
+        for cols in HALVES:
+            nc.vector.tensor_tensor(s[:, cols], numer[:, cols], inv_denom[:, cols], ALU.mult)
+            nc.scalar.activation(p[:, cols], s[:, cols], ACT.Exp)
+        for h in range(2):
+            nc.scalar.activation(inv_p[:, HALVES[h]], s[:, HALVES[h]], ACT.Exp, scale=unit[:])
+            nc.vector.tensor_tensor(
+                ratio[:, HALVES[h]], p[:].indirect(idx4[:, LIST_HALVES[h]]), inv_p[:, HALVES[h]], ALU.mult
+            )
+        nc.scalar.activation(unit[:], unit[:], ACT.Abs_reciprocal_sqrt)
+        for cols in HALVES:
+            nc.scalar.activation(root[:, cols], ratio[:, cols], ACT.Abs_reciprocal_sqrt, bias=unit[:], scale=rival_sb[:])
+
+        faded = pool.tile([P, OUT_CHUNKS, CHUNK], F32, name="faded")
+        mean_r = pool.tile([P, 1], F32, name="mean_r")
+        gain_root = pool.tile([P, 1], F32, name="gain_root")
+        gain = pool.tile([P, 1], F32, name="gain")
+        nc.scalar.activation(
+            faded[:, :, : I // OUT_CHUNKS],
+            root[:].rearrange("p (c n) -> p c n", c=OUT_CHUNKS),
+            ACT.Square,
+            scale=512.0**-0.5,
+            accum_out=mean_r[:],
+        )
+        nc.scalar.activation(gain_root[:], mean_r[:], ACT.Abs_reciprocal_sqrt)
+        nc.scalar.activation(gain[:], gain_root[:], ACT.Square)
+        for h in range(2):
+            nc.vector.tensor_tensor(
+                placed[:].indirect(idx2[:, LIST_HALVES[h]]), root[:, HALVES[h]], root[:, HALVES[h]], ALU.mult
+            )
+        for c in range(OUT_CHUNKS):
+            nc.scalar.activation(faded[:, c, :], old_sb[:, c * CHUNK : (c + 1) * CHUNK], ACT.Copy, scale=fade_sb[:])
+        result = faded[:].rearrange("p c n -> p (c n)")
+        for lo, hi in zip(STORE_EDGES, STORE_EDGES[1:]):
+            nc.vector.scalar_tensor_tensor(result[:, lo:hi], placed[:, lo:hi], gain[:], result[:, lo:hi], ALU.mult, ALU.add)
+            nc.sync.dma_start(out[:, lo:hi], result[:, lo:hi])

@@ -21,7 +21,14 @@ HALF = I // 2
 HALVES = [slice(0, HALF), slice(HALF, I)]
 LIST_HALVES = [slice(0, HALF // 16), slice(HALF // 16, I // 16)]
 OVERLAP = 16
-STAGGERED = [slice(0, HALF + OVERLAP), slice(HALF + OVERLAP, I)]
+
+
+def cut_at(col):
+    return [slice(0, col), slice(col, I)]
+
+
+STAGGERED = cut_at(HALF + OVERLAP)
+STAGGERED_TWICE = cut_at(HALF + 2 * OVERLAP)
 KNEE = 40.0
 OUT_CHUNKS = 4
 CHUNK = M // OUT_CHUNKS
@@ -40,9 +47,14 @@ def tile_attend_saturating_overlinked_counts_kernel(
         idx = lists.tile([P, I // 16], U16, name="idx")
         idx2 = lists.tile([P, I // 16], U16, name="idx2")
         idx4 = lists.tile([P, I // 16], U16, name="idx4")
-        words = pool.tile([P, T], U32, name="words", align_bytes=64, tag="words_then_old")
-        scales = pool.tile([P, T], U8, name="scales", align_bytes=64, tag="bytes_then_words0")
-        q_raw = pool.tile([P, PACK, Q], F32, name="q_raw", tag="query_then_ceil")
+        words = pool.tile([P, T], U32, name="words", align_bytes=64)
+        scales = pool.tile([P, T], U8, name="scales", align_bytes=64, tag="bytes_then_words")
+        q_raw = pool.tile([P, PACK, Q], F32, name="q_raw")
+        half_pts = pool.tile([P, T], F32, name="half_pts")
+        ceilings = pool.tile([P, T], F32, name="ceilings")
+        old_sb = pool.tile([P, M], F32, name="old_sb")
+        rival_sb = pool.tile([P, 1], F32, name="rival_sb")
+        fade_sb = pool.tile([P, 1], F32, name="fade_sb")
         placed = pool.tile([P, M], F32, name="placed")
         zero = pool.tile([P, 1], F32, name="zero")
         unit = pool.tile([P, 1], F32, name="unit")
@@ -53,61 +65,58 @@ def tile_attend_saturating_overlinked_counts_kernel(
         nc.vector.memset(unit[:], -1.0)
         nc.vector.memset(placed[:], 0.0)
 
-        nc.sync.dma_start(idx[:], offs)
-        nc.sync.dma_start(idx4[:], offs4)
-        nc.sync.dma_start(q_raw[:], query.rearrange("(p j) q -> p j q", j=PACK))
-        nc.sync.dma_start(words[:].bitcast(I32), keys_words[0].rearrange("p n t -> p (n t)").bitcast(I32))
-        for quad, queue in enumerate((nc.scalar, nc.scalar, nc.scalar, nc.scalar)):
+        def load_scale_rows(queue, quad):
             queue.dma_start(
                 scales[:].bitcast(I32)[32 * quad : 32 * quad + 4, :],
                 keys_scales[0, 4 * quad : 4 * quad + 4, :].bitcast(I32),
             )
+
+        nc.sync.dma_start(idx[:], offs)
+        nc.sync.dma_start(q_raw[:], query.rearrange("(p j) q -> p j q", j=PACK))
+        for quad, queue in enumerate((nc.scalar, nc.scalar, nc.sync, nc.sync)):
+            load_scale_rows(queue, quad)
+        nc.sync.dma_start(words[:].bitcast(I32), keys_words[0].rearrange("p n t -> p (n t)").bitcast(I32))
+        nc.sync.dma_start(idx4[:], offs4)
         nc.sync.dma_start(idx2[:], offs2)
-        half_pts = pool.tile([P, T], F32, name="half_pts")
         nc.sync.dma_start(half_pts[:], halfp)
+        nc.sync.dma_start(ceilings[:], ceil_t)
+        nc.sync.dma_start(rival_sb[:], rival)
+        nc.sync.dma_start(fade_sb[:], fade)
+        nc.sync.dma_start(old_sb[:], old)
 
         nc.scalar.activation(one[:], zero[:], ACT.Exp)
 
         q_bf = pool.tile([P, Q, PACK], BF16, name="q_bf", align_bytes=64)
         nc.vector.tensor_scalar(q_bf[:], q_raw[:].rearrange("p j q -> p q j"), 2.0, None, ALU.mult)
-        ceilings = pool.tile([P, T], F32, name="ceilings", tag="query_then_ceil")
-        nc.sync.dma_start(ceilings[:], ceil_t)
-        q_codes = pool.tile([P, Q], U32, name="q_codes", align_bytes=64, tag="codes_then_rival")
-        q_scales = pool.tile([P, Q], U8, name="q_scales", align_bytes=64, tag="bytes_then_fade")
+        q_codes = pool.tile([P, Q], U32, name="q_codes", align_bytes=64)
+        q_scales = pool.tile([P, Q], U8, name="q_scales", align_bytes=64)
         k_scales = pool.tile([P, I], U8, name="k_scales", align_bytes=64)
         nc.vector.quantize_mx(
             out=q_codes[:].bitcast(FP8X4), scales=q_scales[:], in_=q_bf[:].rearrange("p q j -> p (q j)")
         )
 
         nc.vector.tensor_copy(k_scales[:], scales[:].indirect(idx[:]))
+        k_words = pool.tile([P, I], U32, name="k_words", align_bytes=64, tag="bytes_then_words")
         x = []
         for h in range(2):
-            k_words = pool.tile([P, HALF], U32, name=f"k_words{h}", align_bytes=64, tag=f"bytes_then_words{h}")
-            nc.vector.tensor_copy(k_words[:], words[:].indirect(idx[:, LIST_HALVES[h]]))
+            nc.vector.tensor_copy(k_words[:, HALVES[h]], words[:].indirect(idx[:, LIST_HALVES[h]]))
             bank = psum.tile([P, HALF], F32, name=f"x{h}")
             nc.tensor.matmul_mx(
                 out=bank[:],
                 lhsT=q_codes[:].bitcast(FP8X4),
                 lhsT_scale=q_scales[:],
-                rhs=k_words[:].bitcast(FP8X4),
+                rhs=k_words[:, HALVES[h]].bitcast(FP8X4),
                 rhs_scale=k_scales[:, HALVES[h]],
                 start=True,
                 stop=True,
             )
             x.append(bank)
 
-        rival_sb = pool.tile([P, 1], F32, name="rival_sb", align_bytes=64, tag="codes_then_rival")
-        fade_sb = pool.tile([P, 1], F32, name="fade_sb", align_bytes=64, tag="bytes_then_fade")
-        nc.sync.dma_start(rival_sb[:], rival)
-        nc.sync.dma_start(fade_sb[:], fade)
-        old_sb = pool.tile([P, M], F32, name="old_sb", align_bytes=64, tag="words_then_old")
-        nc.sync.dma_start(old_sb[:], old)
-
         def slots(name):
             return pool.tile([P, I], F32, name=name)
 
         ex, soft, excess, half_plus, denom = (slots(n) for n in ("ex", "soft", "excess", "half_plus", "denom"))
-        ln_denom, inv_denom, fa, numer, s = (slots(n) for n in ("ln_denom", "inv_denom", "fa", "numer", "s"))
+        ln_denom, inv_denom, numer, s = (slots(n) for n in ("ln_denom", "inv_denom", "numer", "s"))
         p, inv_p, ratio, root = (slots(n) for n in ("p", "inv_p", "ratio", "root"))
 
         for h in range(2):
@@ -119,17 +128,18 @@ def tile_attend_saturating_overlinked_counts_kernel(
             )
         for cols in STAGGERED:
             nc.scalar.activation(soft[:, cols], ex[:, cols], ACT.Ln, bias=one[:])
-        for cols in HALVES:
+        for cols in STAGGERED:
             nc.vector.scalar_tensor_tensor(denom[:, cols], soft[:, cols], KNEE, half_plus[:, cols], ALU.min, ALU.add)
             nc.scalar.activation(ln_denom[:, cols], denom[:, cols], ACT.Ln)
+        fa = half_plus
         nc.vector.scalar_tensor_tensor(fa[:], soft[:], KNEE, excess[:], ALU.min, ALU.add)
         for h in range(2):
             nc.vector.tensor_tensor(
                 numer[:, HALVES[h]], ceilings[:].indirect(idx[:, LIST_HALVES[h]]), fa[:, HALVES[h]], ALU.mult
             )
-        for cols in STAGGERED:
+        for cols in STAGGERED_TWICE:
             nc.scalar.activation(inv_denom[:, cols], ln_denom[:, cols], ACT.Exp, scale=-1.0)
-        for cols in HALVES:
+        for cols in STAGGERED:
             nc.vector.tensor_tensor(s[:, cols], numer[:, cols], inv_denom[:, cols], ALU.mult)
             nc.scalar.activation(p[:, cols], s[:, cols], ACT.Exp)
         for h in range(2):

@@ -56,13 +56,10 @@ def tile_attend_saturating_overlinked_counts_kernel(
         rival_sb = pool.tile([P, 1], F32, name="rival_sb")
         fade_sb = pool.tile([P, 1], F32, name="fade_sb")
         placed = pool.tile([P, M], F32, name="placed")
-        zero = pool.tile([P, 1], F32, name="zero")
-        unit = pool.tile([P, 1], F32, name="unit")
         one = pool.tile([P, 1], F32, name="one")
 
         nc.vector.memset(scales[:].bitcast(I32), 0)
-        nc.vector.memset(zero[:], 0.0)
-        nc.vector.memset(unit[:], -1.0)
+        nc.vector.memset(one[:], 1.0)
         nc.vector.memset(placed[:], 0.0)
 
         def load_scale_rows(queue, quad):
@@ -71,8 +68,8 @@ def tile_attend_saturating_overlinked_counts_kernel(
                 keys_scales[0, 4 * quad : 4 * quad + 4, :].bitcast(I32),
             )
 
-        nc.sync.dma_start(idx[:], offs)
         nc.sync.dma_start(q_raw[:], query.rearrange("(p j) q -> p j q", j=PACK))
+        nc.sync.dma_start(idx[:], offs)
         for quad, queue in enumerate((nc.scalar, nc.scalar, nc.sync, nc.sync)):
             load_scale_rows(queue, quad)
         nc.sync.dma_start(words[:].bitcast(I32), keys_words[0].rearrange("p n t -> p (n t)").bitcast(I32))
@@ -84,18 +81,16 @@ def tile_attend_saturating_overlinked_counts_kernel(
         nc.sync.dma_start(fade_sb[:], fade)
         nc.sync.dma_start(old_sb[:], old)
 
-        nc.scalar.activation(one[:], zero[:], ACT.Exp)
-
         q_bf = pool.tile([P, Q, PACK], BF16, name="q_bf", align_bytes=64)
-        nc.vector.tensor_scalar(q_bf[:], q_raw[:].rearrange("p j q -> p q j"), 2.0, None, ALU.mult)
+        nc.scalar.activation(q_bf[:], q_raw[:].rearrange("p j q -> p q j"), ACT.Copy, scale=2.0)
         q_codes = pool.tile([P, Q], U32, name="q_codes", align_bytes=64)
         q_scales = pool.tile([P, Q], U8, name="q_scales", align_bytes=64)
         k_scales = pool.tile([P, I], U8, name="k_scales", align_bytes=64)
+        nc.vector.tensor_copy(k_scales[:], scales[:].indirect(idx[:]))
         nc.vector.quantize_mx(
             out=q_codes[:].bitcast(FP8X4), scales=q_scales[:], in_=q_bf[:].rearrange("p q j -> p (q j)")
         )
 
-        nc.vector.tensor_copy(k_scales[:], scales[:].indirect(idx[:]))
         k_words = pool.tile([P, I], U32, name="k_words", align_bytes=64, tag="bytes_then_words")
         x = []
         for h in range(2):
@@ -143,13 +138,12 @@ def tile_attend_saturating_overlinked_counts_kernel(
             nc.vector.tensor_tensor(s[:, cols], numer[:, cols], inv_denom[:, cols], ALU.mult)
             nc.scalar.activation(p[:, cols], s[:, cols], ACT.Exp)
         for h in range(2):
-            nc.scalar.activation(inv_p[:, HALVES[h]], s[:, HALVES[h]], ACT.Exp, scale=unit[:])
+            nc.scalar.activation(inv_p[:, HALVES[h]], s[:, HALVES[h]], ACT.Exp, scale=-1.0)
             nc.vector.tensor_tensor(
                 ratio[:, HALVES[h]], p[:].indirect(idx4[:, LIST_HALVES[h]]), inv_p[:, HALVES[h]], ALU.mult
             )
-        nc.scalar.activation(unit[:], unit[:], ACT.Abs_reciprocal_sqrt)
         for cols in HALVES:
-            nc.scalar.activation(root[:, cols], ratio[:, cols], ACT.Abs_reciprocal_sqrt, bias=unit[:], scale=rival_sb[:])
+            nc.scalar.activation(root[:, cols], ratio[:, cols], ACT.Abs_reciprocal_sqrt, bias=one[:], scale=rival_sb[:])
 
         faded = pool.tile([P, OUT_CHUNKS, CHUNK], F32, name="faded")
         mean_r = pool.tile([P, 1], F32, name="mean_r")

@@ -17,22 +17,22 @@ ACT = mybir.ActivationFunctionType
 
 P = 128
 PACK = 4
+PER_COLUMN = 16
+WEIGHT_SCALE = 512.0
+
 HALF = I // 2
 HALVES = [slice(0, HALF), slice(HALF, I)]
-LIST_HALVES = [slice(0, HALF // 16), slice(HALF // 16, I // 16)]
-OVERLAP = 16
+LIST_HALVES = [slice(0, HALF // PER_COLUMN), slice(HALF // PER_COLUMN, I // PER_COLUMN)]
+REACH = 16
+REACH_ONCE = [slice(0, HALF + REACH), slice(HALF + REACH, I)]
+REACH_TWICE = [slice(0, HALF + 2 * REACH), slice(HALF + 2 * REACH, I)]
 
+KNEE = 22.0
+TINY = 2.0**-63
 
-def cut_at(col):
-    return [slice(0, col), slice(col, I)]
-
-
-STAGGERED = cut_at(HALF + OVERLAP)
-STAGGERED_TWICE = cut_at(HALF + 2 * OVERLAP)
-KNEE = 40.0
-OUT_CHUNKS = 4
-CHUNK = M // OUT_CHUNKS
-STORE_EDGES = [0, 256, 768, 1280, 1792, M]
+FADE_CHUNKS = 4
+FADE_COLS = M // FADE_CHUNKS
+STORE_EDGES = [0, 256, 512, 896, 1280, 1664, M]
 
 
 def tile_attend_saturating_overlinked_counts_kernel(
@@ -44,61 +44,60 @@ def tile_attend_saturating_overlinked_counts_kernel(
         pool = ctx.enter_context(tc.tile_pool(name="work", bufs=1))
         psum = ctx.enter_context(tc.psum_pool(name="psum", bufs=1))
 
-        idx = lists.tile([P, I // 16], U16, name="idx")
-        idx2 = lists.tile([P, I // 16], U16, name="idx2")
-        idx4 = lists.tile([P, I // 16], U16, name="idx4")
-        words = pool.tile([P, T], U32, name="words", align_bytes=64)
-        scales = pool.tile([P, T], U8, name="scales", align_bytes=64, tag="bytes_then_words")
+        idx = lists.tile([P, I // PER_COLUMN], U16, name="idx")
+        idx2 = lists.tile([P, I // PER_COLUMN], U16, name="idx2")
+        idx4 = lists.tile([P, I // PER_COLUMN], U16, name="idx4")
+        pool_words = pool.tile([P, T], U32, name="pool_words", align_bytes=64)
+        pool_scales = pool.tile([P, T], U8, name="pool_scales", align_bytes=64, tag="scales_then_words")
         q_raw = pool.tile([P, PACK, Q], F32, name="q_raw")
-        half_pts = pool.tile([P, T], F32, name="half_pts")
-        ceilings = pool.tile([P, T], F32, name="ceilings")
+        pool_half = pool.tile([P, T], F32, name="pool_half")
+        pool_ceil = pool.tile([P, T], F32, name="pool_ceil")
         old_sb = pool.tile([P, M], F32, name="old_sb")
         rival_sb = pool.tile([P, 1], F32, name="rival_sb")
         fade_sb = pool.tile([P, 1], F32, name="fade_sb")
         placed = pool.tile([P, M], F32, name="placed")
         one = pool.tile([P, 1], F32, name="one")
+        tiny = pool.tile([P, 1], F32, name="tiny")
 
-        nc.vector.memset(scales[:].bitcast(I32), 0)
+        nc.vector.memset(pool_scales[:].bitcast(I32), 0)
         nc.vector.memset(one[:], 1.0)
+        nc.vector.memset(tiny[:], TINY)
         nc.vector.memset(placed[:], 0.0)
-
-        def load_scale_rows(queue, quad):
-            queue.dma_start(
-                scales[:].bitcast(I32)[32 * quad : 32 * quad + 4, :],
-                keys_scales[0, 4 * quad : 4 * quad + 4, :].bitcast(I32),
-            )
 
         nc.sync.dma_start(q_raw[:], query.rearrange("(p j) q -> p j q", j=PACK))
         nc.sync.dma_start(idx[:], offs)
-        for quad, queue in enumerate((nc.scalar, nc.scalar, nc.sync, nc.sync)):
-            load_scale_rows(queue, quad)
-        nc.sync.dma_start(words[:].bitcast(I32), keys_words[0].rearrange("p n t -> p (n t)").bitcast(I32))
+        for quadrant, queue in enumerate((nc.scalar, nc.scalar, nc.sync, nc.sync)):
+            queue.dma_start(
+                pool_scales[:].bitcast(I32)[32 * quadrant : 32 * quadrant + 4, :],
+                keys_scales[0, 4 * quadrant : 4 * quadrant + 4, :].bitcast(I32),
+            )
+        nc.sync.dma_start(pool_words[:].bitcast(I32), keys_words[0].rearrange("p n t -> p (n t)").bitcast(I32))
         nc.sync.dma_start(idx4[:], offs4)
         nc.sync.dma_start(idx2[:], offs2)
-        nc.sync.dma_start(half_pts[:], halfp)
-        nc.sync.dma_start(ceilings[:], ceil_t)
+        nc.sync.dma_start(pool_half[:], halfp)
+        nc.sync.dma_start(pool_ceil[:], ceil_t)
         nc.sync.dma_start(rival_sb[:], rival)
         nc.sync.dma_start(fade_sb[:], fade)
         nc.sync.dma_start(old_sb[:], old)
 
         q_bf = pool.tile([P, Q, PACK], BF16, name="q_bf", align_bytes=64)
         nc.scalar.activation(q_bf[:], q_raw[:].rearrange("p j q -> p q j"), ACT.Copy, scale=2.0)
-        q_codes = pool.tile([P, Q], U32, name="q_codes", align_bytes=64)
+        q_words = pool.tile([P, Q], U32, name="q_words", align_bytes=64)
         q_scales = pool.tile([P, Q], U8, name="q_scales", align_bytes=64)
         k_scales = pool.tile([P, I], U8, name="k_scales", align_bytes=64)
-        nc.vector.tensor_copy(k_scales[:], scales[:].indirect(idx[:]))
+        nc.vector.tensor_copy(k_scales[:], pool_scales[:].indirect(idx[:]))
         nc.vector.quantize_mx(
-            out=q_codes[:].bitcast(FP8X4), scales=q_scales[:], in_=q_bf[:].rearrange("p q j -> p (q j)")
+            out=q_words[:].bitcast(FP8X4), scales=q_scales[:], in_=q_bf[:].rearrange("p q j -> p (q j)")
         )
 
-        k_words = pool.tile([P, I], U32, name="k_words", align_bytes=64, tag="bytes_then_words")
+        k_words = pool.tile([P, I], U32, name="k_words", align_bytes=64, tag="scales_then_words")
         x = []
         for h in range(2):
-            nc.vector.tensor_copy(k_words[:, HALVES[h]], words[:].indirect(idx[:, LIST_HALVES[h]]))
+            nc.vector.tensor_copy(k_words[:, HALVES[h]], pool_words[:].indirect(idx[:, LIST_HALVES[h]]))
             bank = psum.tile([P, HALF], F32, name=f"x{h}")
             nc.tensor.matmul_mx(
                 out=bank[:],
-                lhsT=q_codes[:].bitcast(FP8X4),
+                lhsT=q_words[:].bitcast(FP8X4),
                 lhsT_scale=q_scales[:],
                 rhs=k_words[:, HALVES[h]].bitcast(FP8X4),
                 rhs_scale=k_scales[:, HALVES[h]],
@@ -110,61 +109,73 @@ def tile_attend_saturating_overlinked_counts_kernel(
         def slots(name):
             return pool.tile([P, I], F32, name=name)
 
-        ex, soft, excess, half_plus, denom = (slots(n) for n in ("ex", "soft", "excess", "half_plus", "denom"))
-        ln_denom, inv_denom, numer, s = (slots(n) for n in ("ln_denom", "inv_denom", "numer", "s"))
-        p, inv_p, ratio, root = (slots(n) for n in ("p", "inv_p", "ratio", "root"))
-
+        sig, ln_sig, excess, half_excess = slots("sig"), slots("ln_sig"), slots("excess"), slots("half_excess")
+        neg_denom, ln_denom = slots("neg_denom"), slots("ln_denom")
         for h in range(2):
-            nc.scalar.activation(ex[:, HALVES[h]], x[h][:], ACT.Exp)
+            nc.scalar.activation(sig[:, HALVES[h]], x[h][:], ACT.Sigmoid, scale=-1.0)
         for h in range(2):
             nc.vector.tensor_scalar(excess[:, HALVES[h]], x[h][:], -KNEE, 0.0, ALU.add, ALU.max)
             nc.vector.tensor_tensor(
-                half_plus[:, HALVES[h]], half_pts[:].indirect(idx[:, LIST_HALVES[h]]), excess[:, HALVES[h]], ALU.add
+                half_excess[:, HALVES[h]], pool_half[:].indirect(idx[:, LIST_HALVES[h]]), excess[:, HALVES[h]], ALU.add
             )
-        for cols in STAGGERED:
-            nc.scalar.activation(soft[:, cols], ex[:, cols], ACT.Ln, bias=one[:])
-        for cols in STAGGERED:
-            nc.vector.scalar_tensor_tensor(denom[:, cols], soft[:, cols], KNEE, half_plus[:, cols], ALU.min, ALU.add)
-            nc.scalar.activation(ln_denom[:, cols], denom[:, cols], ACT.Ln)
-        fa = half_plus
-        nc.vector.scalar_tensor_tensor(fa[:], soft[:], KNEE, excess[:], ALU.min, ALU.add)
+        for cols in REACH_ONCE:
+            nc.scalar.activation(ln_sig[:, cols], sig[:, cols], ACT.Ln, bias=tiny[:])
+        for cols in REACH_ONCE:
+            nc.vector.scalar_tensor_tensor(
+                neg_denom[:, cols], ln_sig[:, cols], -KNEE, half_excess[:, cols], ALU.max, ALU.subtract
+            )
+            nc.scalar.activation(ln_denom[:, cols], neg_denom[:, cols], ACT.Ln, scale=-1.0)
+
+        neg_fa = half_excess
+        neg_numer, inv_denom, neg_s = slots("neg_numer"), slots("inv_denom"), slots("neg_s")
+        nc.vector.scalar_tensor_tensor(neg_fa[:], ln_sig[:], -KNEE, excess[:], ALU.max, ALU.subtract)
         for h in range(2):
             nc.vector.tensor_tensor(
-                numer[:, HALVES[h]], ceilings[:].indirect(idx[:, LIST_HALVES[h]]), fa[:, HALVES[h]], ALU.mult
+                neg_numer[:, HALVES[h]], pool_ceil[:].indirect(idx[:, LIST_HALVES[h]]), neg_fa[:, HALVES[h]], ALU.mult
             )
-        for cols in STAGGERED_TWICE:
+        for cols in REACH_TWICE:
             nc.scalar.activation(inv_denom[:, cols], ln_denom[:, cols], ACT.Exp, scale=-1.0)
-        for cols in STAGGERED:
-            nc.vector.tensor_tensor(s[:, cols], numer[:, cols], inv_denom[:, cols], ALU.mult)
-            nc.scalar.activation(p[:, cols], s[:, cols], ACT.Exp)
+
+        p, inv_p, ratio, root_r = slots("p"), slots("inv_p"), slots("ratio"), slots("root_r")
+        for cols in REACH_ONCE:
+            nc.vector.tensor_tensor(neg_s[:, cols], neg_numer[:, cols], inv_denom[:, cols], ALU.mult)
+            nc.scalar.activation(p[:, cols], neg_s[:, cols], ACT.Exp, scale=-1.0)
         for h in range(2):
-            nc.scalar.activation(inv_p[:, HALVES[h]], s[:, HALVES[h]], ACT.Exp, scale=-1.0)
+            nc.scalar.activation(inv_p[:, HALVES[h]], neg_s[:, HALVES[h]], ACT.Exp)
             nc.vector.tensor_tensor(
                 ratio[:, HALVES[h]], p[:].indirect(idx4[:, LIST_HALVES[h]]), inv_p[:, HALVES[h]], ALU.mult
             )
         for cols in HALVES:
-            nc.scalar.activation(root[:, cols], ratio[:, cols], ACT.Abs_reciprocal_sqrt, bias=one[:], scale=rival_sb[:])
+            nc.scalar.activation(
+                root_r[:, cols], ratio[:, cols], ACT.Abs_reciprocal_sqrt, bias=one[:], scale=rival_sb[:]
+            )
 
-        faded = pool.tile([P, OUT_CHUNKS, CHUNK], F32, name="faded")
-        mean_r = pool.tile([P, 1], F32, name="mean_r")
-        gain_root = pool.tile([P, 1], F32, name="gain_root")
+        faded = pool.tile([P, FADE_CHUNKS, FADE_COLS], F32, name="faded")
+        sum_scaled = pool.tile([P, 1], F32, name="sum_scaled")
+        root_gain = pool.tile([P, 1], F32, name="root_gain")
         gain = pool.tile([P, 1], F32, name="gain")
         nc.scalar.activation(
-            faded[:, :, : I // OUT_CHUNKS],
-            root[:].rearrange("p (c n) -> p c n", c=OUT_CHUNKS),
+            faded[:, :, : I // FADE_CHUNKS],
+            root_r[:].rearrange("p (c n) -> p c n", c=FADE_CHUNKS),
             ACT.Square,
-            scale=512.0**-0.5,
-            accum_out=mean_r[:],
+            scale=WEIGHT_SCALE**-0.5,
+            accum_out=sum_scaled[:],
         )
-        nc.scalar.activation(gain_root[:], mean_r[:], ACT.Abs_reciprocal_sqrt)
-        nc.scalar.activation(gain[:], gain_root[:], ACT.Square)
+        nc.scalar.activation(root_gain[:], sum_scaled[:], ACT.Abs_reciprocal_sqrt)
+        nc.scalar.activation(gain[:], root_gain[:], ACT.Square)
+
         for h in range(2):
             nc.vector.tensor_tensor(
-                placed[:].indirect(idx2[:, LIST_HALVES[h]]), root[:, HALVES[h]], root[:, HALVES[h]], ALU.mult
+                placed[:].indirect(idx2[:, LIST_HALVES[h]]), root_r[:, HALVES[h]], root_r[:, HALVES[h]], ALU.mult
             )
-        for c in range(OUT_CHUNKS):
-            nc.scalar.activation(faded[:, c, :], old_sb[:, c * CHUNK : (c + 1) * CHUNK], ACT.Copy, scale=fade_sb[:])
+        for c in range(FADE_CHUNKS):
+            nc.scalar.activation(
+                faded[:, c, :], old_sb[:, c * FADE_COLS : (c + 1) * FADE_COLS], ACT.Copy, scale=fade_sb[:]
+            )
+
         result = faded[:].rearrange("p c n -> p (c n)")
         for lo, hi in zip(STORE_EDGES, STORE_EDGES[1:]):
-            nc.vector.scalar_tensor_tensor(result[:, lo:hi], placed[:, lo:hi], gain[:], result[:, lo:hi], ALU.mult, ALU.add)
+            nc.vector.scalar_tensor_tensor(
+                result[:, lo:hi], placed[:, lo:hi], gain[:], result[:, lo:hi], ALU.mult, ALU.add
+            )
             nc.sync.dma_start(out[:, lo:hi], result[:, lo:hi])

from contextlib import ExitStack

import concourse.mybir as mybir

D, T, I, Q, M = 512, 2048, 512, 128, 2048
FLOPS = 2 * D * Q * I

F32 = mybir.dt.float32
BF16 = mybir.dt.bfloat16
I32 = mybir.dt.int32
U32 = mybir.dt.uint32
U16 = mybir.dt.uint16
U8 = mybir.dt.uint8
FP8X4 = mybir.dt.float8_e4m3fn_x4
ALU = mybir.AluOpType
ACT = mybir.ActivationFunctionType

P = 128
PACK = 4
PER_COLUMN = 16
WEIGHT_SCALE = 512.0

HALF = I // 2
HALVES = [slice(0, HALF), slice(HALF, I)]
LIST_HALVES = [slice(0, HALF // PER_COLUMN), slice(HALF // PER_COLUMN, I // PER_COLUMN)]
REACH = 16
REACH_ONCE = [slice(0, HALF + REACH), slice(HALF + REACH, I)]
REACH_TWICE = [slice(0, HALF + 2 * REACH), slice(HALF + 2 * REACH, I)]

KNEE = 22.0
TINY = 2.0**-63

FADE_CHUNKS = 4
FADE_COLS = M // FADE_CHUNKS
STORE_EDGES = [0, 256, 512, 896, 1280, 1664, M]


def tile_attend_saturating_overlinked_counts_kernel(
    tc, query, keys_words, keys_scales, ceil_t, halfp, rival, old, fade, offs, offs2, offs4, out
):
    nc = tc.nc
    with ExitStack() as ctx:
        lists = ctx.enter_context(tc.tile_pool(name="lists", bufs=1))
        pool = ctx.enter_context(tc.tile_pool(name="work", bufs=1))
        psum = ctx.enter_context(tc.psum_pool(name="psum", bufs=1))

        idx = lists.tile([P, I // PER_COLUMN], U16, name="idx")
        idx2 = lists.tile([P, I // PER_COLUMN], U16, name="idx2")
        idx4 = lists.tile([P, I // PER_COLUMN], U16, name="idx4")
        pool_words = pool.tile([P, T], U32, name="pool_words", align_bytes=64)
        pool_scales = pool.tile([P, T], U8, name="pool_scales", align_bytes=64, tag="scales_then_words")
        q_raw = pool.tile([P, PACK, Q], F32, name="q_raw")
        pool_half = pool.tile([P, T], F32, name="pool_half")
        pool_ceil = pool.tile([P, T], F32, name="pool_ceil")
        old_sb = pool.tile([P, M], F32, name="old_sb")
        rival_sb = pool.tile([P, 1], F32, name="rival_sb")
        fade_sb = pool.tile([P, 1], F32, name="fade_sb")
        placed = pool.tile([P, M], F32, name="placed")
        one = pool.tile([P, 1], F32, name="one")
        tiny = pool.tile([P, 1], F32, name="tiny")

        nc.vector.memset(pool_scales[:].bitcast(I32), 0)
        nc.vector.memset(one[:], 1.0)
        nc.vector.memset(tiny[:], TINY)
        nc.vector.memset(placed[:], 0.0)

        nc.sync.dma_start(q_raw[:], query.rearrange("(p j) q -> p j q", j=PACK))
        nc.sync.dma_start(idx[:], offs)
        for quadrant, queue in enumerate((nc.scalar, nc.scalar, nc.sync, nc.sync)):
            queue.dma_start(
                pool_scales[:].bitcast(I32)[32 * quadrant : 32 * quadrant + 4, :],
                keys_scales[0, 4 * quadrant : 4 * quadrant + 4, :].bitcast(I32),
            )
        nc.sync.dma_start(pool_words[:].bitcast(I32), keys_words[0].rearrange("p n t -> p (n t)").bitcast(I32))
        nc.sync.dma_start(idx4[:], offs4)
        nc.sync.dma_start(idx2[:], offs2)
        nc.sync.dma_start(pool_half[:], halfp)
        nc.sync.dma_start(pool_ceil[:], ceil_t)
        nc.sync.dma_start(rival_sb[:], rival)
        nc.sync.dma_start(fade_sb[:], fade)
        nc.sync.dma_start(old_sb[:], old)

        q_bf = pool.tile([P, Q, PACK], BF16, name="q_bf", align_bytes=64)
        nc.scalar.activation(q_bf[:], q_raw[:].rearrange("p j q -> p q j"), ACT.Copy, scale=2.0)
        q_words = pool.tile([P, Q], U32, name="q_words", align_bytes=64)
        q_scales = pool.tile([P, Q], U8, name="q_scales", align_bytes=64)
        k_scales = pool.tile([P, I], U8, name="k_scales", align_bytes=64)
        nc.vector.tensor_copy(k_scales[:], pool_scales[:].indirect(idx[:]))
        nc.vector.quantize_mx(
            out=q_words[:].bitcast(FP8X4), scales=q_scales[:], in_=q_bf[:].rearrange("p q j -> p (q j)")
        )

        k_words = pool.tile([P, I], U32, name="k_words", align_bytes=64, tag="scales_then_words")
        x = []
        for h in range(2):
            nc.vector.tensor_copy(k_words[:, HALVES[h]], pool_words[:].indirect(idx[:, LIST_HALVES[h]]))
            bank = psum.tile([P, HALF], F32, name=f"x{h}")
            nc.tensor.matmul_mx(
                out=bank[:],
                lhsT=q_words[:].bitcast(FP8X4),
                lhsT_scale=q_scales[:],
                rhs=k_words[:, HALVES[h]].bitcast(FP8X4),
                rhs_scale=k_scales[:, HALVES[h]],
                start=True,
                stop=True,
            )
            x.append(bank)

        def slots(name):
            return pool.tile([P, I], F32, name=name)

        sig, ln_sig, excess, half_excess = slots("sig"), slots("ln_sig"), slots("excess"), slots("half_excess")
        neg_denom, ln_denom = slots("neg_denom"), slots("ln_denom")
        for h in range(2):
            nc.scalar.activation(sig[:, HALVES[h]], x[h][:], ACT.Sigmoid, scale=-1.0)
        for h in range(2):
            nc.vector.tensor_scalar(excess[:, HALVES[h]], x[h][:], -KNEE, 0.0, ALU.add, ALU.max)
            nc.vector.tensor_tensor(
                half_excess[:, HALVES[h]], pool_half[:].indirect(idx[:, LIST_HALVES[h]]), excess[:, HALVES[h]], ALU.add
            )
        for cols in REACH_ONCE:
            nc.scalar.activation(ln_sig[:, cols], sig[:, cols], ACT.Ln, bias=tiny[:])
        for cols in REACH_ONCE:
            nc.vector.scalar_tensor_tensor(
                neg_denom[:, cols], ln_sig[:, cols], -KNEE, half_excess[:, cols], ALU.max, ALU.subtract
            )
            nc.scalar.activation(ln_denom[:, cols], neg_denom[:, cols], ACT.Ln, scale=-1.0)

        neg_fa = half_excess
        neg_numer, inv_denom, neg_s = slots("neg_numer"), slots("inv_denom"), slots("neg_s")
        nc.vector.scalar_tensor_tensor(neg_fa[:], ln_sig[:], -KNEE, excess[:], ALU.max, ALU.subtract)
        for h in range(2):
            nc.vector.tensor_tensor(
                neg_numer[:, HALVES[h]], pool_ceil[:].indirect(idx[:, LIST_HALVES[h]]), neg_fa[:, HALVES[h]], ALU.mult
            )
        for cols in REACH_TWICE:
            nc.scalar.activation(inv_denom[:, cols], ln_denom[:, cols], ACT.Exp, scale=-1.0)

        p, inv_p, ratio, root_r = slots("p"), slots("inv_p"), slots("ratio"), slots("root_r")
        for cols in REACH_ONCE:
            nc.vector.tensor_tensor(neg_s[:, cols], neg_numer[:, cols], inv_denom[:, cols], ALU.mult)
            nc.scalar.activation(p[:, cols], neg_s[:, cols], ACT.Exp, scale=-1.0)
        for h in range(2):
            nc.scalar.activation(inv_p[:, HALVES[h]], neg_s[:, HALVES[h]], ACT.Exp)
            nc.vector.tensor_tensor(
                ratio[:, HALVES[h]], p[:].indirect(idx4[:, LIST_HALVES[h]]), inv_p[:, HALVES[h]], ALU.mult
            )
        for cols in HALVES:
            nc.scalar.activation(
                root_r[:, cols], ratio[:, cols], ACT.Abs_reciprocal_sqrt, bias=one[:], scale=rival_sb[:]
            )

        faded = pool.tile([P, FADE_CHUNKS, FADE_COLS], F32, name="faded")
        sum_scaled = pool.tile([P, 1], F32, name="sum_scaled")
        root_gain = pool.tile([P, 1], F32, name="root_gain")
        gain = pool.tile([P, 1], F32, name="gain")
        nc.scalar.activation(
            faded[:, :, : I // FADE_CHUNKS],
            root_r[:].rearrange("p (c n) -> p c n", c=FADE_CHUNKS),
            ACT.Square,
            scale=WEIGHT_SCALE**-0.5,
            accum_out=sum_scaled[:],
        )
        nc.scalar.activation(root_gain[:], sum_scaled[:], ACT.Abs_reciprocal_sqrt)
        nc.scalar.activation(gain[:], root_gain[:], ACT.Square)

        for h in range(2):
            nc.vector.tensor_tensor(
                placed[:].indirect(idx2[:, LIST_HALVES[h]]), root_r[:, HALVES[h]], root_r[:, HALVES[h]], ALU.mult
            )
        for c in range(FADE_CHUNKS):
            nc.scalar.activation(
                faded[:, c, :], old_sb[:, c * FADE_COLS : (c + 1) * FADE_COLS], ACT.Copy, scale=fade_sb[:]
            )

        result = faded[:].rearrange("p c n -> p (c n)")
        for lo, hi in zip(STORE_EDGES, STORE_EDGES[1:]):
            nc.vector.scalar_tensor_tensor(
                result[:, lo:hi], placed[:, lo:hi], gain[:], result[:, lo:hi], ALU.mult, ALU.add
            )
            nc.sync.dma_start(out[:, lo:hi], result[:, lo:hi])
